import numpy as np
import ml_dtypes


def mxq(x, axis, fmt="e4m3"):
    dtype, down = {"e4m3": (ml_dtypes.float8_e4m3fn, 7), "e5m2": (ml_dtypes.float8_e5m2, 14)}[fmt]
    v = np.moveaxis(np.asarray(x, np.float32).astype(ml_dtypes.bfloat16).astype(np.float64), axis, -1)
    blocks = v.reshape(v.shape[:-1] + (-1, 32))
    amax = np.abs(blocks).max(-1, keepdims=True)
    byte = np.maximum(np.where(amax > 0, np.frexp(amax)[1] - 1 + 127, 0) - down, 1)
    scale = np.exp2(byte - 127.0)
    codes = (blocks / scale).astype(np.float32).astype(dtype).astype(np.float64)
    return np.moveaxis((codes * scale).reshape(v.shape), -1, axis)


WIDE = False


def mx_kscale(k):
    if not WIDE:
        return np.ones(k)
    levels = np.array([10, -10, 5, -5, 0])
    if k % 512:
        return np.exp2(np.random.permutation(np.resize(levels, k // 32))).repeat(32)
    a = np.empty((k // 512, 16))
    for p in range(k // 512):
        a[p, :8] = np.random.permutation(np.resize(levels, 8))
        for g in range(8):
            far = levels[np.abs(levels - a[p, g]) >= 10]
            a[p, g + 8] = far[np.random.randint(len(far))]
    return np.exp2(a.ravel()).repeat(32)


def f64(x):
    return np.asarray(x).astype(np.float64)


def striped(idx):
    return np.tile(np.asarray(idx).reshape(-1, 16).T, (8, 1)).astype(np.uint16)


def unstriped(offs):
    return offs[:16].T.reshape(-1).astype(np.int64)


def striped8(idx):
    return np.asarray(idx).reshape(8, -1, 16).transpose(0, 2, 1).reshape(128, -1).astype(np.uint16)


def unstriped8(offs):
    return offs.reshape(8, 16, -1).transpose(0, 2, 1).reshape(8, -1).astype(np.int64)


def pick8(x, idx, run):
    r = np.arange(len(x))
    return x[r[:, None], idx[r % (8 * run) // run]]


E2M1 = np.array([0.0, 0.5, 1.0, 1.5, 2.0, 3.0, 4.0, 6.0, -0.0, -0.5, -1.0, -1.5, -2.0, -3.0, -4.0, -6.0])


def pack_weight(w, fmt):
    k, n = w.shape
    w = f64(np.asarray(w, np.float32).astype(ml_dtypes.bfloat16)).reshape(k // 32, 32, n)
    amax = np.abs(w).max(1)
    if fmt == "e4m3":
        byte = np.frexp(amax)[1] - 1 + 127 - 7
    else:
        mant, ex = np.frexp(amax / 6.0)
        byte = np.where(mant > 0.5, ex, ex - 1) + 127
    byte = np.clip(np.where(amax > 0, byte, 1), 1, 254)
    scaled = (w * np.exp2(127.0 - byte)[:, None, :]).reshape(k, n).astype(np.float32)
    by_word = np.ascontiguousarray(scaled.reshape(k // 512, 128, 4, n).transpose(0, 1, 3, 2))
    if fmt == "e4m3":
        words = by_word.astype(ml_dtypes.float8_e4m3fn).view(np.uint8)
    else:
        c = by_word.astype(ml_dtypes.float4_e2m1fn).view(np.uint8) & 0xF
        words = (c[..., 0::2] | (c[..., 1::2] << 4)).reshape(k // 512, 128, 2 * n)
    return np.ascontiguousarray(words), np.ascontiguousarray(byte.astype(np.uint8).reshape(k // 512, 16, n))


def unpack_weight(words, scales, fmt):
    g, _, n = scales.shape
    words = np.ascontiguousarray(words).reshape(g, 128, n, -1)
    if fmt == "e4m3":
        vals = words.view(ml_dtypes.float8_e4m3fn).astype(np.float64)
    else:
        nib = np.empty((g, 128, n, 4), np.uint8)
        nib[..., 0::2] = words & 0xF
        nib[..., 1::2] = words >> 4
        vals = E2M1[nib]
    vals = vals * np.repeat(np.exp2(scales.astype(np.float64) - 127.0), 8, axis=1)[..., None]
    return vals.transpose(0, 1, 3, 2).reshape(g * 512, n)


K, T, J, R, F, Z, N, C, O = 512, 1024, 256, 512, 512, 1024, 256, 512, 128


def setup_inputs():
    n = np.random.standard_normal
    idx = np.random.permutation(T)[:J]
    idx2 = np.random.permutation(Z)[:J]
    idx3 = np.stack([np.random.permutation(C)[:J] for _ in range(8)])
    idx4 = np.random.permutation(C)[:O]
    idx5 = np.random.permutation(J)[:O]
    ff = mx_kscale(F)
    fk = mx_kscale(K)
    fr = mx_kscale(R)
    xop = pack_weight(n((F, Z)) / ff[:, None], "e4m3")
    wp = pack_weight(n((K, R)) * 1 / np.sqrt(K) / fk[:, None] * fr, "e2m1")
    w2p = pack_weight(n((F, R)) * 1 / np.sqrt(F) * ff[:, None] * fr, "e2m1")
    wbp = pack_weight(n((R, N)) * 1 / np.sqrt(R) / fr[:, None], "e2m1")
    wcp = pack_weight(n((R, N)) * 1 / np.sqrt(R) / fr[:, None], "e4m3")
    return {
        "xo_words": xop[0],
        "xo_scales": xop[1],
        "cq": (np.random.randint(-7, 8, (K, T)).astype(np.float64)).astype(np.float32),
        "gs": (np.random.uniform(0.1, 0.4, (K, 1)) * fk[:, None]).astype(np.float32),
        "w_words": wp[0],
        "w_scales": wp[1],
        "w2_words": w2p[0],
        "w2_scales": w2p[1],
        "wb_words": wbp[0],
        "wb_scales": wbp[1],
        "wc_words": wcp[0],
        "wc_scales": wcp[1],
        "so": (np.random.uniform(0.5, 1.6, (N, 1))).astype(np.float32),
        "sp": (np.random.uniform(0.5, 1.6, (N, 1))).astype(np.float32),
        "offs": striped(idx),
        "offs2": striped(idx2),
        "offs3": striped8(idx3),
        "offs4": striped(idx4),
        "offs5": striped(idx5),
    }


def reference(xo_words, xo_scales, cq, gs, w_words, w_scales, w2_words, w2_scales, wb_words, wb_scales, wc_words, wc_scales, so, sp, offs, offs2, offs3, offs4, offs5):
    idx = unstriped(offs)
    idx2 = unstriped(offs2)
    idx3 = unstriped8(offs3)
    idx4 = unstriped(offs4)
    idx5 = unstriped(offs5)
    xou = unpack_weight(xo_words, xo_scales, "e4m3")
    wu = unpack_weight(w_words, w_scales, "e2m1")
    w2u = unpack_weight(w2_words, w2_scales, "e2m1")
    wbu = unpack_weight(wb_words, wb_scales, "e2m1")
    wcu = unpack_weight(wc_words, wc_scales, "e4m3")
    x1 = f64(cq)[:, idx] * f64(gs)
    x1q = mxq(x1, 0, "e4m3")
    a = wu.T @ x1q
    xoidx2g = xou[:, idx2]
    b = w2u.T @ xoidx2g
    hid = np.maximum(a, b)
    hidq = mxq(hid, 0, "e4m3")
    p = wbu.T @ hidq
    q = wcu.T @ hidq
    pw = np.zeros((N, C))
    pw[np.arange(N)[:, None], idx3[np.arange(N) % 128 // 16]] = p
    y = pw[:, idx4] * f64(so) - q[:, idx5] * f64(sp)
    return y

@@ -1,0 +1,211 @@
+from contextlib import ExitStack
+
+import concourse.mybir as mybir
+
+K, T, J, R, F, Z, N, C, O = 512, 1024, 256, 512, 512, 1024, 256, 512, 128
+FLOPS = 2 * (K * R * J + F * R * J + 2 * R * N * J)
+
+F32 = mybir.dt.float32
+BF16 = mybir.dt.bfloat16
+I32 = mybir.dt.int32
+U32 = mybir.dt.uint32
+U16 = mybir.dt.uint16
+U8 = mybir.dt.uint8
+E4M3X4 = mybir.dt.float8_e4m3fn_x4
+E2M1X4 = mybir.dt.float4_e2m1fn_x4
+COPY = mybir.ActivationFunctionType.Copy
+ALU = mybir.AluOpType
+
+P = 128
+PACK = 4
+HALF = J // 2
+LIST_COLS = HALF // 16
+
+
+def tile_list_outcomeownboard_codednote_kernel(
+    tc, xo_words, xo_scales, cq, gs, w_words, w_scales, w2_words, w2_scales, wb_words, wb_scales,
+    wc_words, wc_scales, so, sp, offs, offs2, offs3, offs4, offs5, out,
+):
+    nc = tc.nc
+    with ExitStack() as ctx:
+        lists = ctx.enter_context(tc.tile_pool(name="lists", bufs=1))
+        sb = ctx.enter_context(tc.tile_pool(name="sb", bufs=1))
+        ps = ctx.enter_context(tc.psum_pool(name="ps", bufs=1))
+
+        def tile(name, shape, dtype):
+            return sb.tile(shape, dtype, name=name, align_bytes=64)
+
+        def scale_plane(name, width):
+            plane = tile(name, [P, width], U8)
+            nc.vector.memset(plane[:].bitcast(I32), 0)
+            return plane
+
+        def load_scale_rows(plane, scales):
+            rows = scales[0].bitcast(I32)
+            for r in range(4):
+                nc.sync.dma_start(plane[r:P:32, :].bitcast(I32), rows[r:16:4, :])
+
+        def load_list(name, src):
+            t = lists.tile(list(src.shape), U16, name=name)
+            nc.sync.dma_start(t[:], src)
+            return t
+
+        def load_bytes(name, src):
+            t = tile(name, [P, src.shape[1]], U8)
+            nc.sync.dma_start(t[:].bitcast(I32), src.bitcast(I32))
+            return t
+
+        cq_planes = cq.rearrange("(p t) c -> t p c", t=PACK)
+
+        def load_cq(t):
+            plane = tile("cq%d" % t, [P, T], F32)
+            nc.sync.dma_start(plane[:], cq_planes[t])
+            return plane
+
+        w_sc = scale_plane("w_sc", R)
+        xo_sc = scale_plane("xo_sc", Z)
+        w2_sc = scale_plane("w2_sc", R)
+        wb_sc = scale_plane("wb_sc", N)
+        wc_sc = scale_plane("wc_sc", N)
+        board = [tile("board%d" % n, [P, C], F32) for n in range(2)]
+        for n in range(2):
+            nc.vector.memset(board[n][:], 0.0)
+
+        cq_t = [load_cq(0)]
+        idx = load_list("idx", offs)
+        gs_t = tile("gs_t", [P, PACK], F32)
+        nc.sync.dma_start(gs_t[:], gs.rearrange("(p t) one -> p (t one)", t=PACK))
+        cq_t.append(load_cq(1))
+        w_raw = load_bytes("w_raw", w_words[0])
+        load_scale_rows(w_sc, w_scales)
+        cq_t.append(load_cq(2))
+        idx2 = load_list("idx2", offs2)
+        load_scale_rows(xo_sc, xo_scales)
+        cq_t.append(load_cq(3))
+        load_scale_rows(w2_sc, w2_scales)
+        w2_raw = load_bytes("w2_raw", w2_words[0])
+        xo_w = load_bytes("xo_w", xo_words[0].rearrange("p c r -> p (c r)"))
+        wb_w = load_bytes("wb_w", wb_words[0])
+        load_scale_rows(wb_sc, wb_scales)
+        idx3 = load_list("idx3", offs3)
+        wc_w = load_bytes("wc_w", wc_words[0].rearrange("p c r -> p (c r)"))
+        load_scale_rows(wc_sc, wc_scales)
+        idx4 = load_list("idx4", offs4)
+        idx5 = load_list("idx5", offs5)
+        so_t = tile("so_t", [P, 2], F32)
+        sp_t = tile("sp_t", [P, 2], F32)
+        with nc.allow_non_contiguous_dma(reason="one weight a partition for each of two row tiles"):
+            nc.sync.dma_start(so_t[:], so.rearrange("(n p) one -> p (n one)", p=P))
+            nc.sync.dma_start(sp_t[:], sp.rearrange("(n p) one -> p (n one)", p=P))
+
+        def deal(name, words, plane):
+            dealt_words = tile(name + "_words", [P, 2 * R], U8)
+            dealt_plane = tile(name + "_plane", [P, R], U8)
+            nc.vector.tensor_copy(
+                dealt_plane[:].rearrange("p (t m) -> p t m", t=PACK),
+                plane[:].rearrange("p (m t) -> p t m", t=PACK),
+            )
+            nc.vector.tensor_copy(
+                dealt_words[:].bitcast(U16).rearrange("p (t m) -> p t m", t=PACK),
+                words[:].bitcast(U16).rearrange("p (m t) -> p t m", t=PACK),
+            )
+            return dealt_words, dealt_plane
+
+        def first_stage(name, weights, codes, plane):
+            dealt_words, dealt_plane = weights
+            acc = ps.tile([P, PACK, HALF], F32, name=name)
+            for t in range(PACK):
+                nc.tensor.matmul_mx(
+                    acc[:, t, :],
+                    lhsT=dealt_words[:, 2 * P * t : 2 * P * (t + 1)].bitcast(E2M1X4),
+                    lhsT_scale=dealt_plane[:, P * t : P * (t + 1)],
+                    rhs=codes.bitcast(E4M3X4),
+                    rhs_scale=plane,
+                    start=True,
+                    stop=True,
+                )
+            return acc
+
+        halves = [slice(HALF * h, HALF * (h + 1)) for h in range(2)]
+        list_halves = [slice(LIST_COLS * h, LIST_COLS * (h + 1)) for h in range(2)]
+
+        w_dealt = deal("w", w_raw, w_sc)
+        xo_plane = tile("xo_plane", [P, J], U8)
+        nc.vector.tensor_copy(xo_plane[:], xo_sc[:].indirect(idx2[:]))
+        w2_dealt = deal("w2", w2_raw, w2_sc)
+
+        x1 = tile("x1", [P, PACK, J], BF16)
+        for t in range(PACK):
+            nc.scalar.activation(x1[:, t, :], cq_t[t][:].indirect(idx[:]), COPY, scale=gs_t[:, t : t + 1])
+        woven = []
+        for h in range(2):
+            x1_woven = tile("x1_woven%d" % h, [P, HALF, PACK], BF16)
+            nc.vector.tensor_copy(
+                x1_woven[:].rearrange("p (c i) t -> p c t i", i=4),
+                x1[:, :, halves[h]].rearrange("p t (c i) -> p c t i", i=4),
+            )
+            woven.append(x1_woven)
+        a_sb = []
+        for h in range(2):
+            codes = tile("x1_codes%d" % h, [P, HALF], U32)
+            plane = tile("x1_plane%d" % h, [P, HALF], U8)
+            nc.vector.quantize_mx(codes[:].bitcast(E4M3X4), plane[:], woven[h][:].rearrange("p j t -> p (j t)"))
+            a_ps = first_stage("a%d" % h, w_dealt, codes[:], plane[:])
+            a_woven = tile("a_woven%d" % h, [P, HALF, PACK], F32)
+            nc.scalar.copy(a_woven[:], a_ps[:].rearrange("p t j -> p j t"))
+            a_sb.append(a_woven)
+
+        b_ps = []
+        for h in range(2):
+            codes = tile("xo_codes%d" % h, [P, HALF], U32)
+            nc.vector.tensor_copy(codes[:], xo_w[:].bitcast(U32).indirect(idx2[:, list_halves[h]]))
+            b_ps.append(first_stage("b%d" % h, w2_dealt, codes[:], xo_plane[:, halves[h]]))
+
+        hid_codes = tile("hid_codes", [P, J], U32)
+        hid_plane = tile("hid_plane", [P, J], U8)
+        for h in range(2):
+            hid = tile("hid%d" % h, [P, HALF, PACK], BF16)
+            nc.vector.tensor_tensor(hid[:], b_ps[h][:].rearrange("p t j -> p j t"), a_sb[h][:], ALU.max)
+            nc.vector.quantize_mx(
+                hid_codes[:, halves[h]].bitcast(E4M3X4), hid_plane[:, halves[h]], hid[:].rearrange("p j t -> p (j t)")
+            )
+            p_ps = ps.tile([P, 2, HALF], F32, name="p%d" % h)
+            for n in range(2):
+                nc.tensor.matmul_mx(
+                    p_ps[:, n, :],
+                    lhsT=wb_w[:, 2 * P * n : 2 * P * (n + 1)].bitcast(E2M1X4),
+                    lhsT_scale=wb_sc[:, P * n : P * (n + 1)],
+                    rhs=hid_codes[:, halves[h]].bitcast(E4M3X4),
+                    rhs_scale=hid_plane[:, halves[h]],
+                    start=True,
+                    stop=True,
+                )
+            p_sb = tile("p_sb%d" % h, [P, 2, HALF], F32)
+            if h == 0:
+                nc.scalar.copy(p_sb[:], p_ps[:])
+            else:
+                nc.vector.tensor_copy(p_sb[:], p_ps[:])
+            for n in range(2):
+                nc.scalar.activation(board[n][:].indirect(idx3[:, list_halves[h]]), p_sb[:, n, :], COPY)
+
+        q_ps = ps.tile([P, 2, J], F32, name="q")
+        for n in range(2):
+            nc.tensor.matmul_mx(
+                q_ps[:, n, :],
+                lhsT=wc_w[:, 4 * P * n : 4 * P * (n + 1)].bitcast(E4M3X4),
+                lhsT_scale=wc_sc[:, P * n : P * (n + 1)],
+                rhs=hid_codes[:].bitcast(E4M3X4),
+                rhs_scale=hid_plane[:],
+                start=True,
+                stop=True,
+            )
+        for n in range(2):
+            q_sb = tile("q_sb%d" % n, [P, J], F32)
+            nc.vector.tensor_copy(q_sb[:], q_ps[:, n, :])
+            q_pick = tile("q_pick%d" % n, [P, O], F32)
+            nc.scalar.activation(q_pick[:], q_sb[:].indirect(idx5[:]), COPY, scale=sp_t[:, n : n + 1])
+            board_pick = tile("board_pick%d" % n, [P, O], F32)
+            nc.scalar.activation(board_pick[:], board[n][:].indirect(idx4[:]), COPY, scale=so_t[:, n : n + 1])
+            y = tile("y%d" % n, [P, O], F32)
+            nc.vector.tensor_tensor(y[:], board_pick[:], q_pick[:], ALU.subtract)
+            nc.sync.dma_start(out[P * n : P * (n + 1), :], y[:])

@@ -32,8 +32,8 @@ def tile_list_outcomeownboard_codednote_kernel(
         sb = ctx.enter_context(tc.tile_pool(name="sb", bufs=1))
         ps = ctx.enter_context(tc.psum_pool(name="ps", bufs=1))
 
-        def tile(name, shape, dtype):
-            return sb.tile(shape, dtype, name=name, align_bytes=64)
+        def tile(name, shape, dtype, tag=None):
+            return sb.tile(shape, dtype, name=name, tag=tag or name, align_bytes=64)
 
         def scale_plane(name, width):
             plane = tile(name, [P, width], U8)
@@ -164,15 +164,19 @@ def tile_list_outcomeownboard_codednote_kernel(
         hid_codes = tile("hid_codes", [P, J], U32)
         hid_plane = tile("hid_plane", [P, J], U8)
         for h in range(2):
-            hid = tile("hid%d" % h, [P, HALF, PACK], BF16)
+            hid = tile("hid%d" % h, [P, HALF, PACK], BF16, tag="hid")
             nc.vector.tensor_tensor(hid[:], b_ps[h][:].rearrange("p t j -> p j t"), a_sb[h][:], ALU.max)
             nc.vector.quantize_mx(
                 hid_codes[:, halves[h]].bitcast(E4M3X4), hid_plane[:, halves[h]], hid[:].rearrange("p j t -> p (j t)")
             )
-            p_ps = ps.tile([P, 2, HALF], F32, name="p%d" % h)
+            if h == 0:
+                p_ps = [ps.tile([P, HALF], F32, name="p0%d" % n)[:] for n in range(2)]
+            else:
+                p_both = ps.tile([P, 2, HALF], F32, name="p1")
+                p_ps = [p_both[:, n, :] for n in range(2)]
             for n in range(2):
                 nc.tensor.matmul_mx(
-                    p_ps[:, n, :],
+                    p_ps[n],
                     lhsT=wb_w[:, 2 * P * n : 2 * P * (n + 1)].bitcast(E2M1X4),
                     lhsT_scale=wb_sc[:, P * n : P * (n + 1)],
                     rhs=hid_codes[:, halves[h]].bitcast(E4M3X4),
@@ -182,9 +186,10 @@ def tile_list_outcomeownboard_codednote_kernel(
                 )
             p_sb = tile("p_sb%d" % h, [P, 2, HALF], F32)
             if h == 0:
-                nc.scalar.copy(p_sb[:], p_ps[:])
+                for n in range(2):
+                    nc.scalar.copy(p_sb[:, n, :], p_ps[n])
             else:
-                nc.vector.tensor_copy(p_sb[:], p_ps[:])
+                nc.vector.tensor_copy(p_sb[:], p_both[:])
             for n in range(2):
                 nc.scalar.activation(board[n][:].indirect(idx3[:, list_halves[h]]), p_sb[:, n, :], COPY)
 

from contextlib import ExitStack

import concourse.mybir as mybir

K, T, J, R, F, Z, N, C, O = 512, 1024, 256, 512, 512, 1024, 256, 512, 128
FLOPS = 2 * (K * R * J + F * R * J + 2 * R * N * J)

F32 = mybir.dt.float32
BF16 = mybir.dt.bfloat16
I32 = mybir.dt.int32
U32 = mybir.dt.uint32
U16 = mybir.dt.uint16
U8 = mybir.dt.uint8
E4M3X4 = mybir.dt.float8_e4m3fn_x4
E2M1X4 = mybir.dt.float4_e2m1fn_x4
COPY = mybir.ActivationFunctionType.Copy
ALU = mybir.AluOpType

P = 128
PACK = 4
HALF = J // 2
LIST_COLS = HALF // 16


def tile_list_outcomeownboard_codednote_kernel(
    tc, xo_words, xo_scales, cq, gs, w_words, w_scales, w2_words, w2_scales, wb_words, wb_scales,
    wc_words, wc_scales, so, sp, offs, offs2, offs3, offs4, offs5, out,
):
    nc = tc.nc
    with ExitStack() as ctx:
        lists = ctx.enter_context(tc.tile_pool(name="lists", bufs=1))
        sb = ctx.enter_context(tc.tile_pool(name="sb", bufs=1))
        ps = ctx.enter_context(tc.psum_pool(name="ps", bufs=1))

        def tile(name, shape, dtype, tag=None):
            return sb.tile(shape, dtype, name=name, tag=tag or name, align_bytes=64)

        def scale_plane(name, width):
            plane = tile(name, [P, width], U8)
            nc.vector.memset(plane[:].bitcast(I32), 0)
            return plane

        def load_scale_rows(plane, scales):
            rows = scales[0].bitcast(I32)
            for r in range(4):
                nc.sync.dma_start(plane[r:P:32, :].bitcast(I32), rows[r:16:4, :])

        def load_list(name, src):
            t = lists.tile(list(src.shape), U16, name=name)
            nc.sync.dma_start(t[:], src)
            return t

        def load_bytes(name, src):
            t = tile(name, [P, src.shape[1]], U8)
            nc.sync.dma_start(t[:].bitcast(I32), src.bitcast(I32))
            return t

        cq_planes = cq.rearrange("(p t) c -> t p c", t=PACK)

        def load_cq(t):
            plane = tile("cq%d" % t, [P, T], F32)
            nc.sync.dma_start(plane[:], cq_planes[t])
            return plane

        w_sc = scale_plane("w_sc", R)
        xo_sc = scale_plane("xo_sc", Z)
        w2_sc = scale_plane("w2_sc", R)
        wb_sc = scale_plane("wb_sc", N)
        wc_sc = scale_plane("wc_sc", N)
        board = [tile("board%d" % n, [P, C], F32) for n in range(2)]
        for n in range(2):
            nc.vector.memset(board[n][:], 0.0)

        cq_t = [load_cq(0)]
        idx = load_list("idx", offs)
        gs_t = tile("gs_t", [P, PACK], F32)
        nc.sync.dma_start(gs_t[:], gs.rearrange("(p t) one -> p (t one)", t=PACK))
        cq_t.append(load_cq(1))
        w_raw = load_bytes("w_raw", w_words[0])
        load_scale_rows(w_sc, w_scales)
        cq_t.append(load_cq(2))
        idx2 = load_list("idx2", offs2)
        load_scale_rows(xo_sc, xo_scales)
        cq_t.append(load_cq(3))
        load_scale_rows(w2_sc, w2_scales)
        w2_raw = load_bytes("w2_raw", w2_words[0])
        xo_w = load_bytes("xo_w", xo_words[0].rearrange("p c r -> p (c r)"))
        wb_w = load_bytes("wb_w", wb_words[0])
        load_scale_rows(wb_sc, wb_scales)
        idx3 = load_list("idx3", offs3)
        wc_w = load_bytes("wc_w", wc_words[0].rearrange("p c r -> p (c r)"))
        load_scale_rows(wc_sc, wc_scales)
        idx4 = load_list("idx4", offs4)
        idx5 = load_list("idx5", offs5)
        so_t = tile("so_t", [P, 2], F32)
        sp_t = tile("sp_t", [P, 2], F32)
        with nc.allow_non_contiguous_dma(reason="one weight a partition for each of two row tiles"):
            nc.sync.dma_start(so_t[:], so.rearrange("(n p) one -> p (n one)", p=P))
            nc.sync.dma_start(sp_t[:], sp.rearrange("(n p) one -> p (n one)", p=P))

        def deal(name, words, plane):
            dealt_words = tile(name + "_words", [P, 2 * R], U8)
            dealt_plane = tile(name + "_plane", [P, R], U8)
            nc.vector.tensor_copy(
                dealt_plane[:].rearrange("p (t m) -> p t m", t=PACK),
                plane[:].rearrange("p (m t) -> p t m", t=PACK),
            )
            nc.vector.tensor_copy(
                dealt_words[:].bitcast(U16).rearrange("p (t m) -> p t m", t=PACK),
                words[:].bitcast(U16).rearrange("p (m t) -> p t m", t=PACK),
            )
            return dealt_words, dealt_plane

        def first_stage(name, weights, codes, plane):
            dealt_words, dealt_plane = weights
            acc = ps.tile([P, PACK, HALF], F32, name=name)
            for t in range(PACK):
                nc.tensor.matmul_mx(
                    acc[:, t, :],
                    lhsT=dealt_words[:, 2 * P * t : 2 * P * (t + 1)].bitcast(E2M1X4),
                    lhsT_scale=dealt_plane[:, P * t : P * (t + 1)],
                    rhs=codes.bitcast(E4M3X4),
                    rhs_scale=plane,
                    start=True,
                    stop=True,
                )
            return acc

        halves = [slice(HALF * h, HALF * (h + 1)) for h in range(2)]
        list_halves = [slice(LIST_COLS * h, LIST_COLS * (h + 1)) for h in range(2)]

        w_dealt = deal("w", w_raw, w_sc)
        xo_plane = tile("xo_plane", [P, J], U8)
        nc.vector.tensor_copy(xo_plane[:], xo_sc[:].indirect(idx2[:]))
        w2_dealt = deal("w2", w2_raw, w2_sc)

        x1 = tile("x1", [P, PACK, J], BF16)
        for t in range(PACK):
            nc.scalar.activation(x1[:, t, :], cq_t[t][:].indirect(idx[:]), COPY, scale=gs_t[:, t : t + 1])
        woven = []
        for h in range(2):
            x1_woven = tile("x1_woven%d" % h, [P, HALF, PACK], BF16)
            nc.vector.tensor_copy(
                x1_woven[:].rearrange("p (c i) t -> p c t i", i=4),
                x1[:, :, halves[h]].rearrange("p t (c i) -> p c t i", i=4),
            )
            woven.append(x1_woven)
        a_sb = []
        for h in range(2):
            codes = tile("x1_codes%d" % h, [P, HALF], U32)
            plane = tile("x1_plane%d" % h, [P, HALF], U8)
            nc.vector.quantize_mx(codes[:].bitcast(E4M3X4), plane[:], woven[h][:].rearrange("p j t -> p (j t)"))
            a_ps = first_stage("a%d" % h, w_dealt, codes[:], plane[:])
            a_woven = tile("a_woven%d" % h, [P, HALF, PACK], F32)
            nc.scalar.copy(a_woven[:], a_ps[:].rearrange("p t j -> p j t"))
            a_sb.append(a_woven)

        b_ps = []
        for h in range(2):
            codes = tile("xo_codes%d" % h, [P, HALF], U32)
            nc.vector.tensor_copy(codes[:], xo_w[:].bitcast(U32).indirect(idx2[:, list_halves[h]]))
            b_ps.append(first_stage("b%d" % h, w2_dealt, codes[:], xo_plane[:, halves[h]]))

        hid_codes = tile("hid_codes", [P, J], U32)
        hid_plane = tile("hid_plane", [P, J], U8)
        for h in range(2):
            hid = tile("hid%d" % h, [P, HALF, PACK], BF16, tag="hid")
            nc.vector.tensor_tensor(hid[:], b_ps[h][:].rearrange("p t j -> p j t"), a_sb[h][:], ALU.max)
            nc.vector.quantize_mx(
                hid_codes[:, halves[h]].bitcast(E4M3X4), hid_plane[:, halves[h]], hid[:].rearrange("p j t -> p (j t)")
            )
            if h == 0:
                p_ps = [ps.tile([P, HALF], F32, name="p0%d" % n)[:] for n in range(2)]
            else:
                p_both = ps.tile([P, 2, HALF], F32, name="p1")
                p_ps = [p_both[:, n, :] for n in range(2)]
            for n in range(2):
                nc.tensor.matmul_mx(
                    p_ps[n],
                    lhsT=wb_w[:, 2 * P * n : 2 * P * (n + 1)].bitcast(E2M1X4),
                    lhsT_scale=wb_sc[:, P * n : P * (n + 1)],
                    rhs=hid_codes[:, halves[h]].bitcast(E4M3X4),
                    rhs_scale=hid_plane[:, halves[h]],
                    start=True,
                    stop=True,
                )
            p_sb = tile("p_sb%d" % h, [P, 2, HALF], F32)
            if h == 0:
                for n in range(2):
                    nc.scalar.copy(p_sb[:, n, :], p_ps[n])
            else:
                nc.vector.tensor_copy(p_sb[:], p_both[:])
            for n in range(2):
                nc.scalar.activation(board[n][:].indirect(idx3[:, list_halves[h]]), p_sb[:, n, :], COPY)

        q_ps = ps.tile([P, 2, J], F32, name="q")
        for n in range(2):
            nc.tensor.matmul_mx(
                q_ps[:, n, :],
                lhsT=wc_w[:, 4 * P * n : 4 * P * (n + 1)].bitcast(E4M3X4),
                lhsT_scale=wc_sc[:, P * n : P * (n + 1)],
                rhs=hid_codes[:].bitcast(E4M3X4),
                rhs_scale=hid_plane[:],
                start=True,
                stop=True,
            )
        for n in range(2):
            q_sb = tile("q_sb%d" % n, [P, J], F32)
            nc.vector.tensor_copy(q_sb[:], q_ps[:, n, :])
            q_pick = tile("q_pick%d" % n, [P, O], F32)
            nc.scalar.activation(q_pick[:], q_sb[:].indirect(idx5[:]), COPY, scale=sp_t[:, n : n + 1])
            board_pick = tile("board_pick%d" % n, [P, O], F32)
            nc.scalar.activation(board_pick[:], board[n][:].indirect(idx4[:]), COPY, scale=so_t[:, n : n + 1])
            y = tile("y%d" % n, [P, O], F32)
            nc.vector.tensor_tensor(y[:], board_pick[:], q_pick[:], ALU.subtract)
            nc.sync.dma_start(out[P * n : P * (n + 1), :], y[:])
